import numpy as np
import ml_dtypes


def mxq(x, axis, fmt="e4m3"):
    dtype, down = {"e4m3": (ml_dtypes.float8_e4m3fn, 7), "e5m2": (ml_dtypes.float8_e5m2, 14)}[fmt]
    v = np.moveaxis(np.asarray(x, np.float32).astype(ml_dtypes.bfloat16).astype(np.float64), axis, -1)
    blocks = v.reshape(v.shape[:-1] + (-1, 32))
    amax = np.abs(blocks).max(-1, keepdims=True)
    byte = np.maximum(np.where(amax > 0, np.frexp(amax)[1] - 1 + 127, 0) - down, 1)
    scale = np.exp2(byte - 127.0)
    codes = (blocks / scale).astype(np.float32).astype(dtype).astype(np.float64)
    return np.moveaxis((codes * scale).reshape(v.shape), -1, axis)


WIDE = False


def mx_kscale(k):
    if not WIDE:
        return np.ones(k)
    levels = np.array([10, -10, 5, -5, 0])
    if k % 512:
        return np.exp2(np.random.permutation(np.resize(levels, k // 32))).repeat(32)
    a = np.empty((k // 512, 16))
    for p in range(k // 512):
        a[p, :8] = np.random.permutation(np.resize(levels, 8))
        for g in range(8):
            far = levels[np.abs(levels - a[p, g]) >= 10]
            a[p, g + 8] = far[np.random.randint(len(far))]
    return np.exp2(a.ravel()).repeat(32)


def f64(x):
    return np.asarray(x).astype(np.float64)


def striped(idx):
    return np.tile(np.asarray(idx).reshape(-1, 16).T, (8, 1)).astype(np.uint16)


def unstriped(offs):
    return offs[:16].T.reshape(-1).astype(np.int64)


E2M1 = np.array([0.0, 0.5, 1.0, 1.5, 2.0, 3.0, 4.0, 6.0, -0.0, -0.5, -1.0, -1.5, -2.0, -3.0, -4.0, -6.0])


def pack_weight(w, fmt):
    k, n = w.shape
    w = f64(np.asarray(w, np.float32).astype(ml_dtypes.bfloat16)).reshape(k // 32, 32, n)
    amax = np.abs(w).max(1)
    if fmt == "e4m3":
        byte = np.frexp(amax)[1] - 1 + 127 - 7
    else:
        mant, ex = np.frexp(amax / 6.0)
        byte = np.where(mant > 0.5, ex, ex - 1) + 127
    byte = np.clip(np.where(amax > 0, byte, 1), 1, 254)
    scaled = (w * np.exp2(127.0 - byte)[:, None, :]).reshape(k, n).astype(np.float32)
    by_word = np.ascontiguousarray(scaled.reshape(k // 512, 128, 4, n).transpose(0, 1, 3, 2))
    if fmt == "e4m3":
        words = by_word.astype(ml_dtypes.float8_e4m3fn).view(np.uint8)
    else:
        c = by_word.astype(ml_dtypes.float4_e2m1fn).view(np.uint8) & 0xF
        words = (c[..., 0::2] | (c[..., 1::2] << 4)).reshape(k // 512, 128, 2 * n)
    return np.ascontiguousarray(words), np.ascontiguousarray(byte.astype(np.uint8).reshape(k // 512, 16, n))


def unpack_weight(words, scales, fmt):
    g, _, n = scales.shape
    words = np.ascontiguousarray(words).reshape(g, 128, n, -1)
    if fmt == "e4m3":
        vals = words.view(ml_dtypes.float8_e4m3fn).astype(np.float64)
    else:
        nib = np.empty((g, 128, n, 4), np.uint8)
        nib[..., 0::2] = words & 0xF
        nib[..., 1::2] = words >> 4
        vals = E2M1[nib]
    vals = vals * np.repeat(np.exp2(scales.astype(np.float64) - 127.0), 8, axis=1)[..., None]
    return vals.transpose(0, 1, 3, 2).reshape(g * 512, n)


def sigmoid(v):
    return 1.0 / (1.0 + np.exp(-v))


def bf(x):
    return np.asarray(x, np.float32).astype(ml_dtypes.bfloat16)


def planes(Y):
    r, m = Y.shape
    b = f64(bf(Y)).reshape(r // 32, 32, m)
    amax = np.abs(b).max(1)
    byte = np.clip(np.where(amax > 0, np.frexp(amax)[1] - 1 + 127 - 7, 1), 1, 254)
    codes = (b * np.exp2(127.0 - byte)[:, None, :]).reshape(r, m).astype(np.float32).astype(ml_dtypes.float8_e4m3fn).view(np.uint8)
    words = codes.reshape(r // 512, 128, 4, m).transpose(0, 1, 3, 2)
    return np.ascontiguousarray(words), np.ascontiguousarray(byte.astype(np.uint8).reshape(r // 512, 16, m))


D, T, I, Q, E = 512, 1024, 512, 256, 512


def setup_inputs():
    n = np.random.standard_normal
    idx = np.random.permutation(T)[:I]
    idx2 = np.random.permutation(T)[:I]
    fd = mx_kscale(D)
    fi = mx_kscale(I)
    keysp = pack_weight(n((D, T)) / fd[:, None], "e2m1")
    return {
        "query": (n((D, Q)) * 1.0 / np.sqrt(D) * fd[:, None]).astype(np.float32),
        "keys_words": keysp[0],
        "keys_scales": keysp[1],
        "bias": (np.random.uniform(-1.0, 1.0, (I, 1))).astype(np.float32),
        "vals": (n((E, T)) * np.random.uniform(0.3, 1.5, (1, T))).astype(np.float32),
        "half": (np.random.uniform(0.3, 2.0, (I, 1))).astype(np.float32),
        "us": (np.random.uniform(0.02, 0.1, (I, 1)) * fi[:, None]).astype(np.float32),
        "vsc": (np.random.uniform(0.5, 2.0, (I, 1)) / fi[:, None]).astype(np.float32),
        "offs": striped(idx),
        "offs2": striped(idx2),
    }


def reference(query, keys_words, keys_scales, bias, vals, half, us, vsc, offs, offs2):
    idx = unstriped(offs)
    idx2 = unstriped(offs2)
    keysu = unpack_weight(keys_words, keys_scales, "e2m1")
    keysidxg = keysu[:, idx]
    queryq = mxq(f64(query), 0, "e4m3")
    a = keysidxg.T @ queryq
    va = f64(vals)[:, idx].T
    vb = f64(vals)[:, idx2].T
    nv = np.mean(np.square(va - vb), axis=1, keepdims=True)
    nf = nv / (nv + f64(half)) * f64(us)
    w = sigmoid(a + f64(bias)) * nf
    vv = va * f64(vsc)
    vvq = mxq(vv, 0, "e4m3")
    wq = mxq(w, 0, "e4m3")
    o = vvq.T @ wq
    words, scales = planes(o)
    return o, words, scales

@@ -1,0 +1,210 @@
+from contextlib import ExitStack
+
+import concourse.mybir as mybir
+from concourse.masks import make_identity
+
+D, T, I, Q, E = 512, 1024, 512, 256, 512
+FLOPS = 2 * D * I * Q + 2 * I * E * Q
+
+F32 = mybir.dt.float32
+BF16 = mybir.dt.bfloat16
+I32 = mybir.dt.int32
+U32 = mybir.dt.uint32
+U16 = mybir.dt.uint16
+U8 = mybir.dt.uint8
+FP8X4 = mybir.dt.float8_e4m3fn_x4
+FP4X4 = mybir.dt.float4_e2m1fn_x4
+ALU = mybir.AluOpType
+ACT = mybir.ActivationFunctionType
+
+P = 128
+PACK = 4
+HALVES = 2
+QH = Q // HALVES
+
+
+def tile_attend_noveltyread_pl_kernel(tc, query, keys_words, keys_scales, bias, vals, half, us, vsc, offs, offs2, out_0, out_1, out_2):
+    nc = tc.nc
+    with ExitStack() as ctx:
+        held = ctx.enter_context(tc.tile_pool(name="held", bufs=1))
+        ring = ctx.enter_context(tc.tile_pool(name="ring", bufs=2))
+        psum = ctx.enter_context(tc.psum_pool(name="psum", bufs=1))
+        psum2 = ctx.enter_context(tc.psum_pool(name="psum2", bufs=2))
+
+        list_a = held.tile([P, I // 16], U16, name="list_a")
+        list_b = held.tile([P, I // 16], U16, name="list_b")
+        key_scales = held.tile([P, T], U8, name="key_scales")
+        key_words = held.tile([P, T], U16, name="key_words")
+        pool_rows = [held.tile([P, T], F32, name=f"pool_rows{j}") for j in range(PACK)]
+        query_raw = held.tile([P, PACK, Q], F32, name="query_raw")
+        bias_t = held.tile([P, PACK], F32, name="bias_t")
+        half_t = held.tile([P, PACK], F32, name="half_t")
+        us_t = held.tile([P, PACK], F32, name="us_t")
+        vsc_t = held.tile([P, PACK], F32, name="vsc_t")
+        ident = held.tile([P, P], F32, name="ident")
+        warm_in = held.tile([P, 1], F32, name="warm_in")
+        warm_out = held.tile([P, 1], F32, name="warm_out")
+
+        vals_dealt = vals.rearrange("(p j) t -> p j t", j=PACK)
+
+        def by_slot(vec):
+            return vec.rearrange("(p t) o -> p (t o)", t=PACK)
+
+        nc.vector.memset(key_scales[:].bitcast(I32), 0)
+        nc.vector.memset(warm_in[:], 0.0)
+        nc.sync.dma_start(list_a[:], offs)
+        for quad in range(4):
+            nc.scalar.dma_start(
+                key_scales[32 * quad : 32 * quad + 4, :].bitcast(I32),
+                keys_scales[0, 4 * quad : 4 * quad + 4, :].bitcast(I32),
+            )
+        nc.scalar.activation(warm_out[:], warm_in[:], ACT.Sigmoid)
+        nc.sync.dma_start(pool_rows[0][:], vals_dealt[:, 0, :])
+        nc.sync.dma_start(list_b[:], offs2)
+        nc.sync.dma_start(vsc_t[:], by_slot(vsc))
+        nc.sync.dma_start(query_raw[:], query.rearrange("(p j) q -> p j q", j=PACK))
+        for j in range(1, PACK):
+            nc.sync.dma_start(pool_rows[j][:], vals_dealt[:, j, :])
+        nc.sync.dma_start(key_words[:].bitcast(I32), keys_words[0].bitcast(I32))
+        nc.sync.dma_start(bias_t[:], by_slot(bias))
+        nc.sync.dma_start(half_t[:], by_slot(half))
+        nc.sync.dma_start(us_t[:], by_slot(us))
+        make_identity(nc, ident[:])
+
+        scales_listed = held.tile([P, I], U8, name="scales_listed")
+        nc.vector.tensor_copy(scales_listed[:], key_scales[:].indirect(list_a[:]))
+
+        query_bf = held.tile([P, Q, PACK], BF16, name="query_bf", align_bytes=64)
+        nc.scalar.copy(
+            query_bf[:].rearrange("p (c i) j -> p c j i", i=4),
+            query_raw[:].rearrange("p j (c i) -> p c j i", i=4),
+        )
+
+        squares_sum = psum.tile([P, PACK, P], F32, name="squares_sum")
+        vv_bf = []
+        for j in range(PACK):
+            va = ring.tile([P, I], F32, name="va")
+            nc.vector.tensor_copy(va[:], pool_rows[j][:].indirect(list_a[:]))
+            diff = ring.tile([P, I], F32, name="diff")
+            nc.vector.tensor_tensor(diff[:], pool_rows[j][:].indirect(list_b[:]), va[:], ALU.subtract)
+
+            va_turned = psum2.tile([P, PACK, P], F32, name="va_turned")
+            for t in range(PACK):
+                nc.tensor.transpose(va_turned[:, t, :], va[:, t::PACK], ident[:])
+
+            squares = ring.tile([P, PACK, P], F32, name="squares")
+            nc.scalar.activation(
+                squares[:].rearrange("p t s -> p s t"),
+                diff[:].rearrange("p (s t) -> p s t", t=PACK),
+                ACT.Square,
+            )
+            for t in range(PACK):
+                nc.tensor.matmul(
+                    squares_sum[:, t, :], squares[:, t, :], ident[:], is_transpose=True,
+                    start=(j == 0 and t == 0), stop=(j == PACK - 1 and t == PACK - 1),
+                )
+
+            pairs = ring.tile([P, 2, P, 2], BF16, name="pairs")
+            for t in range(PACK):
+                nc.scalar.activation(pairs[:, t // 2, :, t % 2], va_turned[:, t, :], ACT.Copy, scale=vsc_t[:, t : t + 1])
+            woven = held.tile([P, P * PACK], BF16, name=f"vv_bf{j}", align_bytes=64)
+            nc.scalar.copy(
+                woven[:].bitcast(F32).rearrange("p (e u) -> p e u", u=2),
+                pairs[:].rearrange("p u e r -> p u (e r)").bitcast(F32).rearrange("p u e -> p e u"),
+            )
+            vv_bf.append(woven)
+
+        words_listed = held.tile([P, I], U16, name="words_listed")
+        nc.vector.tensor_copy(words_listed[:], key_words[:].indirect(list_a[:]))
+        words_dealt = held.tile([P, PACK, P], U16, name="words_dealt", align_bytes=64)
+        nc.vector.tensor_copy(words_dealt[:], words_listed[:].rearrange("p (s t) -> p t s", t=PACK))
+        scales_dealt = held.tile([P, PACK, P], U8, name="scales_dealt", align_bytes=64)
+        nc.vector.tensor_copy(scales_dealt[:], scales_listed[:].rearrange("p (s t) -> p t s", t=PACK))
+
+        query_codes = held.tile([P, Q], U32, name="query_codes", align_bytes=64)
+        query_scales = held.tile([P, Q], U8, name="query_scales", align_bytes=64)
+        nc.vector.quantize_mx(query_codes[:].bitcast(FP8X4), query_scales[:], query_bf[:].rearrange("p q j -> p (q j)"))
+
+        sig = []
+        for h in range(HALVES):
+            cols = slice(h * QH, (h + 1) * QH)
+            scores = psum.tile([P, PACK, QH], F32, name=f"scores{h}")
+            for t in range(PACK):
+                nc.tensor.matmul_mx(
+                    scores[:, t, :],
+                    lhsT=words_dealt[:, t, :].bitcast(FP4X4), lhsT_scale=scales_dealt[:, t, :],
+                    rhs=query_codes[:, cols].bitcast(FP8X4), rhs_scale=query_scales[:, cols],
+                    start=True, stop=True,
+                )
+            gate = held.tile([P, PACK, QH], F32, name=f"gate{h}")
+            for t in range(PACK):
+                nc.scalar.activation(gate[:, t, :], scores[:, t, :], ACT.Sigmoid, bias=bias_t[:, t : t + 1])
+            sig.append(gate)
+
+        total = held.tile([P, PACK], F32, name="total")
+        nc.vector.tensor_reduce(total[:], squares_sum[:], mybir.AxisListType.X, ALU.add)
+        den = held.tile([P, PACK], F32, name="den")
+        nc.vector.scalar_tensor_tensor(den[:], total[:], 1.0 / E, half_t[:], ALU.mult, ALU.add)
+        num = held.tile([P, PACK], F32, name="num")
+        nc.vector.scalar_tensor_tensor(num[:], total[:], 1.0 / E, us_t[:], ALU.mult, ALU.mult)
+        rec = held.tile([P, PACK], F32, name="rec")
+        nc.vector.reciprocal(rec[:], den[:])
+        nf = held.tile([P, PACK], F32, name="nf")
+        nc.vector.tensor_tensor(nf[:], num[:], rec[:], ALU.mult)
+
+        vv_codes, vv_scales = [], []
+        for j in range(PACK):
+            codes = held.tile([P, P], U32, name=f"vv_codes{j}", align_bytes=64)
+            scales = held.tile([P, P], U8, name=f"vv_scales{j}", align_bytes=64)
+            nc.vector.quantize_mx(codes[:].bitcast(FP8X4), scales[:], vv_bf[j][:])
+            vv_codes.append(codes)
+            vv_scales.append(scales)
+
+        w_bf = []
+        for h in range(HALVES):
+            w = held.tile([P, QH, PACK], BF16, name=f"w_bf{h}", align_bytes=64)
+            nc.vector.tensor_tensor(
+                w[:].rearrange("p (c i) t -> p c t i", i=4),
+                sig[h][:].rearrange("p t (c i) -> p c t i", i=4),
+                nf[:].unsqueeze(1).unsqueeze(3).to_broadcast([P, QH // 4, PACK, 4]),
+                ALU.mult,
+            )
+            w_bf.append(w)
+
+        out_dealt = out_0.rearrange("(p j) q -> p j q", j=PACK)
+        out_words = out_1[0].rearrange("p c r -> p (c r)").bitcast(I32)
+        out_scales = held.tile([P, Q], U8, name="out_scales", align_bytes=64)
+        results = []
+        for h in range(HALVES):
+            w_codes = held.tile([P, QH], U32, name=f"w_codes{h}", align_bytes=64)
+            w_scales = held.tile([P, QH], U8, name=f"w_scales{h}", align_bytes=64)
+            nc.vector.quantize_mx(w_codes[:].bitcast(FP8X4), w_scales[:], w_bf[h][:].rearrange("p q t -> p (q t)"))
+            acc = psum.tile([P, PACK, QH], F32, name=f"acc{h}")
+            for j in range(PACK):
+                nc.tensor.matmul_mx(
+                    acc[:, j, :],
+                    lhsT=vv_codes[j][:].bitcast(FP8X4), lhsT_scale=vv_scales[j][:],
+                    rhs=w_codes[:].bitcast(FP8X4), rhs_scale=w_scales[:],
+                    start=True, stop=True,
+                )
+            result = held.tile([P, PACK, QH], F32, name=f"result{h}")
+            nc.scalar.copy(result[:], acc[:])
+            nc.sync.dma_start(out_dealt[:, :, h * QH : (h + 1) * QH], result[:])
+            results.append(result)
+
+        for h in range(HALVES):
+            cols = slice(h * QH, (h + 1) * QH)
+            out_bf = held.tile([P, QH, PACK], BF16, name=f"out_bf{h}", align_bytes=64)
+            nc.vector.tensor_copy(
+                out_bf[:].rearrange("p (c i) j -> p c j i", i=4),
+                results[h][:].rearrange("p j (c i) -> p c j i", i=4),
+            )
+            out_codes = held.tile([P, QH], U32, name=f"out_codes{h}", align_bytes=64)
+            nc.vector.quantize_mx(out_codes[:].bitcast(FP8X4), out_scales[:, cols], out_bf[:].rearrange("p q j -> p (q j)"))
+            nc.sync.dma_start(out_words[:, cols], out_codes[:].bitcast(I32))
+        for quad in range(4):
+            queue = nc.sync if quad % 2 == 0 else nc.scalar
+            queue.dma_start(
+                out_2[0, 4 * quad : 4 * quad + 4, :].bitcast(I32),
+                out_scales[32 * quad : 32 * quad + 4, :].bitcast(I32),
+            )

@@ -35,7 +35,7 @@ def tile_attend_noveltyread_pl_kernel(tc, query, keys_words, keys_scales, bias, 
         list_b = held.tile([P, I // 16], U16, name="list_b")
         key_scales = held.tile([P, T], U8, name="key_scales")
         key_words = held.tile([P, T], U16, name="key_words")
-        pool_rows = [held.tile([P, T], F32, name=f"pool_rows{j}") for j in range(PACK)]
+        pool_rows = [held.tile([P, T], F32, name=f"pool_rows{j}", tag=f"pool_rows{j}", align_bytes=64) for j in range(PACK)]
         query_raw = held.tile([P, PACK, Q], F32, name="query_raw")
         bias_t = held.tile([P, PACK], F32, name="bias_t")
         half_t = held.tile([P, PACK], F32, name="half_t")
@@ -50,14 +50,10 @@ def tile_attend_noveltyread_pl_kernel(tc, query, keys_words, keys_scales, bias, 
         def by_slot(vec):
             return vec.rearrange("(p t) o -> p (t o)", t=PACK)
 
-        nc.vector.memset(key_scales[:].bitcast(I32), 0)
+        nc.gpsimd.memset(key_scales[:].bitcast(I32), 0)
         nc.vector.memset(warm_in[:], 0.0)
         nc.sync.dma_start(list_a[:], offs)
-        for quad in range(4):
-            nc.scalar.dma_start(
-                key_scales[32 * quad : 32 * quad + 4, :].bitcast(I32),
-                keys_scales[0, 4 * quad : 4 * quad + 4, :].bitcast(I32),
-            )
+        nc.sync.dma_start(key_words[:].bitcast(I32), keys_words[0].bitcast(I32))
         nc.scalar.activation(warm_out[:], warm_in[:], ACT.Sigmoid)
         nc.sync.dma_start(pool_rows[0][:], vals_dealt[:, 0, :])
         nc.sync.dma_start(list_b[:], offs2)
@@ -65,14 +61,18 @@ def tile_attend_noveltyread_pl_kernel(tc, query, keys_words, keys_scales, bias, 
         nc.sync.dma_start(query_raw[:], query.rearrange("(p j) q -> p j q", j=PACK))
         for j in range(1, PACK):
             nc.sync.dma_start(pool_rows[j][:], vals_dealt[:, j, :])
-        nc.sync.dma_start(key_words[:].bitcast(I32), keys_words[0].bitcast(I32))
+        for quad in range(4):
+            nc.sync.dma_start(
+                key_scales[32 * quad : 32 * quad + 4, :].bitcast(I32),
+                keys_scales[0, 4 * quad : 4 * quad + 4, :].bitcast(I32),
+            )
         nc.sync.dma_start(bias_t[:], by_slot(bias))
         nc.sync.dma_start(half_t[:], by_slot(half))
         nc.sync.dma_start(us_t[:], by_slot(us))
         make_identity(nc, ident[:])
 
-        scales_listed = held.tile([P, I], U8, name="scales_listed")
-        nc.vector.tensor_copy(scales_listed[:], key_scales[:].indirect(list_a[:]))
+        words_listed = held.tile([P, I], U16, name="words_listed")
+        nc.vector.tensor_copy(words_listed[:], key_words[:].indirect(list_a[:]))
 
         query_bf = held.tile([P, Q, PACK], BF16, name="query_bf", align_bytes=64)
         nc.scalar.copy(
@@ -80,19 +80,24 @@ def tile_attend_noveltyread_pl_kernel(tc, query, keys_words, keys_scales, bias, 
             query_raw[:].rearrange("p j (c i) -> p c j i", i=4),
         )
 
-        squares_sum = psum.tile([P, PACK, P], F32, name="squares_sum")
-        vv_bf = []
+        squares_sum = [psum.tile([P, 2, P], F32, name=f"squares_sum{u}") for u in range(2)]
+        vv_bf = held.tile([P, PACK, P * PACK], BF16, name="vv_bf", align_bytes=64)
+        total = held.tile([P, PACK], F32, name="total")
+        summed = held.tile([P, 2, P], F32, name="summed")
         for j in range(PACK):
-            va = ring.tile([P, I], F32, name="va")
+            va = held.tile([P, I], F32, name=f"va{j}", tag=f"va{j}", align_bytes=64)
             nc.vector.tensor_copy(va[:], pool_rows[j][:].indirect(list_a[:]))
-            diff = ring.tile([P, I], F32, name="diff")
+            diff = held.tile([P, I], F32, name=f"diff{j}", tag=f"diff{j}", align_bytes=64)
             nc.vector.tensor_tensor(diff[:], pool_rows[j][:].indirect(list_b[:]), va[:], ALU.subtract)
 
-            va_turned = psum2.tile([P, PACK, P], F32, name="va_turned")
+            va_turned = psum2.tile([P, PACK, P], F32, name="va_turned", tag="va_turned")
             for t in range(PACK):
                 nc.tensor.transpose(va_turned[:, t, :], va[:, t::PACK], ident[:])
 
-            squares = ring.tile([P, PACK, P], F32, name="squares")
+            if j < PACK - 1:
+                squares = ring.tile([P, PACK, P], F32, name="squares")
+            else:
+                squares = held.tile([P, PACK, P], F32, name="last_squares", tag="last_squares", align_bytes=64)
             nc.scalar.activation(
                 squares[:].rearrange("p t s -> p s t"),
                 diff[:].rearrange("p (s t) -> p s t", t=PACK),
@@ -100,49 +105,63 @@ def tile_attend_noveltyread_pl_kernel(tc, query, keys_words, keys_scales, bias, 
             )
             for t in range(PACK):
                 nc.tensor.matmul(
-                    squares_sum[:, t, :], squares[:, t, :], ident[:], is_transpose=True,
-                    start=(j == 0 and t == 0), stop=(j == PACK - 1 and t == PACK - 1),
+                    squares_sum[t // 2][:, t % 2, :], squares[:, t, :], ident[:], is_transpose=True,
+                    start=(j == 0 and t % 2 == 0), stop=(j == PACK - 1 and t % 2 == 1),
                 )
 
-            pairs = ring.tile([P, 2, P, 2], BF16, name="pairs")
+            if j < PACK - 1:
+                pairs = ring.tile([P, 2, P, 2], BF16, name="pairs")
+            else:
+                pairs = held.tile([P, 2, P, 2], BF16, name="last_pairs", tag="diff3", align_bytes=64)
             for t in range(PACK):
                 nc.scalar.activation(pairs[:, t // 2, :, t % 2], va_turned[:, t, :], ACT.Copy, scale=vsc_t[:, t : t + 1])
-            woven = held.tile([P, P * PACK], BF16, name=f"vv_bf{j}", align_bytes=64)
+            if j == PACK - 1:
+                for t in range(2):
+                    nc.scalar.activation(summed[:, t, :], squares_sum[0][:, t, :], ACT.Copy, accum_out=total[:, t : t + 1])
             nc.scalar.copy(
-                woven[:].bitcast(F32).rearrange("p (e u) -> p e u", u=2),
+                vv_bf[:, j, :].bitcast(F32).rearrange("p (e u) -> p e u", u=2),
                 pairs[:].rearrange("p u e r -> p u (e r)").bitcast(F32).rearrange("p u e -> p e u"),
             )
-            vv_bf.append(woven)
 
-        words_listed = held.tile([P, I], U16, name="words_listed")
-        nc.vector.tensor_copy(words_listed[:], key_words[:].indirect(list_a[:]))
-        words_dealt = held.tile([P, PACK, P], U16, name="words_dealt", align_bytes=64)
-        nc.vector.tensor_copy(words_dealt[:], words_listed[:].rearrange("p (s t) -> p t s", t=PACK))
-        scales_dealt = held.tile([P, PACK, P], U8, name="scales_dealt", align_bytes=64)
-        nc.vector.tensor_copy(scales_dealt[:], scales_listed[:].rearrange("p (s t) -> p t s", t=PACK))
-
-        query_codes = held.tile([P, Q], U32, name="query_codes", align_bytes=64)
+        scales_listed = held.tile([P, I], U8, name="scales_listed", tag="va3", align_bytes=64)
+        nc.vector.tensor_copy(scales_listed[:], key_scales[:].indirect(list_a[:]))
+        query_codes = held.tile([P, Q], U32, name="query_codes", tag="diff2", align_bytes=64)
         query_scales = held.tile([P, Q], U8, name="query_scales", align_bytes=64)
         nc.vector.quantize_mx(query_codes[:].bitcast(FP8X4), query_scales[:], query_bf[:].rearrange("p q j -> p (q j)"))
+        words_dealt = held.tile([P, PACK, P], U16, name="words_dealt", tag="pool_rows3", align_bytes=64)
+        nc.vector.tensor_copy(words_dealt[:], words_listed[:].rearrange("p (s t) -> p t s", t=PACK))
+        scales_dealt = held.tile([P, PACK, P], U8, name="scales_dealt", tag="last_squares", align_bytes=64)
+        nc.vector.tensor_copy(scales_dealt[:], scales_listed[:].rearrange("p (s t) -> p t s", t=PACK))
 
         sig = []
         for h in range(HALVES):
             cols = slice(h * QH, (h + 1) * QH)
-            scores = psum.tile([P, PACK, QH], F32, name=f"scores{h}")
+            if h == 0:
+                scores = [psum.tile([P, QH], F32, name=f"scores0_{t}")[:] for t in range(PACK)]
+            else:
+                shared = psum2.tile([P, PACK, QH], F32, name="scores1", tag="va_turned")
+                scores = [shared[:, t, :] for t in range(PACK)]
             for t in range(PACK):
                 nc.tensor.matmul_mx(
-                    scores[:, t, :],
+                    scores[t],
                     lhsT=words_dealt[:, t, :].bitcast(FP4X4), lhsT_scale=scales_dealt[:, t, :],
                     rhs=query_codes[:, cols].bitcast(FP8X4), rhs_scale=query_scales[:, cols],
                     start=True, stop=True,
                 )
             gate = held.tile([P, PACK, QH], F32, name=f"gate{h}")
             for t in range(PACK):
-                nc.scalar.activation(gate[:, t, :], scores[:, t, :], ACT.Sigmoid, bias=bias_t[:, t : t + 1])
+                nc.scalar.activation(gate[:, t, :], scores[t], ACT.Sigmoid, bias=bias_t[:, t : t + 1])
             sig.append(gate)
 
-        total = held.tile([P, PACK], F32, name="total")
-        nc.vector.tensor_reduce(total[:], squares_sum[:], mybir.AxisListType.X, ALU.add)
+        nc.vector.tensor_reduce(total[:, 2:4], squares_sum[1][:], mybir.AxisListType.X, ALU.add)
+        vv_codes = held.tile([P, PACK, P], U32, name="vv_codes", align_bytes=64)
+        vv_scales = held.tile([P, PACK, P], U8, name="vv_scales", align_bytes=64)
+        nc.vector.quantize_mx(
+            vv_codes[:].rearrange("p j e -> p (j e)").bitcast(FP8X4),
+            vv_scales[:].rearrange("p j e -> p (j e)"),
+            vv_bf[:].rearrange("p j x -> p (j x)"),
+        )
+
         den = held.tile([P, PACK], F32, name="den")
         nc.vector.scalar_tensor_tensor(den[:], total[:], 1.0 / E, half_t[:], ALU.mult, ALU.add)
         num = held.tile([P, PACK], F32, name="num")
@@ -151,14 +170,6 @@ def tile_attend_noveltyread_pl_kernel(tc, query, keys_words, keys_scales, bias, 
         nc.vector.reciprocal(rec[:], den[:])
         nf = held.tile([P, PACK], F32, name="nf")
         nc.vector.tensor_tensor(nf[:], num[:], rec[:], ALU.mult)
-
-        vv_codes, vv_scales = [], []
-        for j in range(PACK):
-            codes = held.tile([P, P], U32, name=f"vv_codes{j}", align_bytes=64)
-            scales = held.tile([P, P], U8, name=f"vv_scales{j}", align_bytes=64)
-            nc.vector.quantize_mx(codes[:].bitcast(FP8X4), scales[:], vv_bf[j][:])
-            vv_codes.append(codes)
-            vv_scales.append(scales)
 
         w_bf = []
         for h in range(HALVES):
@@ -179,11 +190,11 @@ def tile_attend_noveltyread_pl_kernel(tc, query, keys_words, keys_scales, bias, 
             w_codes = held.tile([P, QH], U32, name=f"w_codes{h}", align_bytes=64)
             w_scales = held.tile([P, QH], U8, name=f"w_scales{h}", align_bytes=64)
             nc.vector.quantize_mx(w_codes[:].bitcast(FP8X4), w_scales[:], w_bf[h][:].rearrange("p q t -> p (q t)"))
-            acc = psum.tile([P, PACK, QH], F32, name=f"acc{h}")
+            acc = psum2.tile([P, PACK, QH], F32, name=f"acc{h}", tag="va_turned")
             for j in range(PACK):
                 nc.tensor.matmul_mx(
                     acc[:, j, :],
-                    lhsT=vv_codes[j][:].bitcast(FP8X4), lhsT_scale=vv_scales[j][:],
+                    lhsT=vv_codes[:, j, :].bitcast(FP8X4), lhsT_scale=vv_scales[:, j, :],
                     rhs=w_codes[:].bitcast(FP8X4), rhs_scale=w_scales[:],
                     start=True, stop=True,
                 )

@@ -27,7 +27,6 @@ def tile_attend_noveltyread_pl_kernel(tc, query, keys_words, keys_scales, bias, 
     nc = tc.nc
     with ExitStack() as ctx:
         held = ctx.enter_context(tc.tile_pool(name="held", bufs=1))
-        ring = ctx.enter_context(tc.tile_pool(name="ring", bufs=2))
         psum = ctx.enter_context(tc.psum_pool(name="psum", bufs=1))
         psum2 = ctx.enter_context(tc.psum_pool(name="psum2", bufs=2))
 
@@ -36,7 +35,7 @@ def tile_attend_noveltyread_pl_kernel(tc, query, keys_words, keys_scales, bias, 
         key_scales = held.tile([P, T], U8, name="key_scales")
         key_words = held.tile([P, T], U16, name="key_words")
         pool_rows = [held.tile([P, T], F32, name=f"pool_rows{j}", tag=f"pool_rows{j}", align_bytes=64) for j in range(PACK)]
-        query_raw = held.tile([P, PACK, Q], F32, name="query_raw")
+        query_raw = held.tile([P, PACK, Q], F32, name="query_raw", tag="query_raw", align_bytes=64)
         bias_t = held.tile([P, PACK], F32, name="bias_t")
         half_t = held.tile([P, PACK], F32, name="half_t")
         us_t = held.tile([P, PACK], F32, name="us_t")
@@ -57,8 +56,8 @@ def tile_attend_noveltyread_pl_kernel(tc, query, keys_words, keys_scales, bias, 
         nc.scalar.activation(warm_out[:], warm_in[:], ACT.Sigmoid)
         nc.sync.dma_start(pool_rows[0][:], vals_dealt[:, 0, :])
         nc.sync.dma_start(list_b[:], offs2)
-        nc.sync.dma_start(vsc_t[:], by_slot(vsc))
         nc.sync.dma_start(query_raw[:], query.rearrange("(p j) q -> p j q", j=PACK))
+        nc.sync.dma_start(vsc_t[:], by_slot(vsc))
         for j in range(1, PACK):
             nc.sync.dma_start(pool_rows[j][:], vals_dealt[:, j, :])
         for quad in range(4):
@@ -84,20 +83,33 @@ def tile_attend_noveltyread_pl_kernel(tc, query, keys_words, keys_scales, bias, 
         vv_bf = held.tile([P, PACK, P * PACK], BF16, name="vv_bf", align_bytes=64)
         total = held.tile([P, PACK], F32, name="total")
         summed = held.tile([P, 2, P], F32, name="summed")
-        for j in range(PACK):
-            va = held.tile([P, I], F32, name=f"va{j}", tag=f"va{j}", align_bytes=64)
-            nc.vector.tensor_copy(va[:], pool_rows[j][:].indirect(list_a[:]))
-            diff = held.tile([P, I], F32, name=f"diff{j}", tag=f"diff{j}", align_bytes=64)
-            nc.vector.tensor_tensor(diff[:], pool_rows[j][:].indirect(list_b[:]), va[:], ALU.subtract)
+        listed, turned = {}, {}
 
-            va_turned = psum2.tile([P, PACK, P], F32, name="va_turned", tag="va_turned")
+        def gather_values(j):
+            listed[j] = held.tile([P, I], F32, name=f"va{j}", tag=f"va{j}", align_bytes=64)
+            nc.vector.tensor_copy(listed[j][:], pool_rows[j][:].indirect(list_a[:]))
+            turned[j] = psum2.tile([P, PACK, P], F32, name=f"va_turned{j}", tag="va_turned")
             for t in range(PACK):
-                nc.tensor.transpose(va_turned[:, t, :], va[:, t::PACK], ident[:])
+                nc.tensor.transpose(turned[j][:, t, :], listed[j][:, t::PACK], ident[:])
 
-            if j < PACK - 1:
-                squares = ring.tile([P, PACK, P], F32, name="squares")
-            else:
-                squares = held.tile([P, PACK, P], F32, name="last_squares", tag="last_squares", align_bytes=64)
+        def scale_and_weave(j, between):
+            planes = held.tile([P, PACK, P], BF16, name=f"planes{j}", tag=("planes0", "planes1", "planes2", "pool_rows2")[j], align_bytes=64)
+            for t in range(PACK):
+                nc.scalar.activation(planes[:, t, :], turned[j][:, t, :], ACT.Copy, scale=vsc_t[:, t : t + 1])
+            for t in between:
+                nc.scalar.activation(summed[:, t, :], squares_sum[0][:, t, :], ACT.Copy, accum_out=total[:, t : t + 1])
+            nc.scalar.copy(
+                vv_bf[:, j, :].rearrange("p (c i t) -> p c t i", i=4, t=PACK),
+                planes[:].rearrange("p t (c i) -> p c t i", i=4),
+            )
+
+        def novelty_part(j):
+            diff = held.tile([P, I], F32, name=f"diff{j}", tag=("diff0", "planes0", "pool_rows1", "pool_rows2")[j], align_bytes=64)
+            nc.vector.tensor_tensor(diff[:], pool_rows[j][:].indirect(list_b[:]), listed[j][:], ALU.subtract)
+            squares = held.tile(
+                [P, PACK, P], F32, name=f"squares{j}",
+                tag=("query_raw", "planes2", "planes0", "pool_rows1")[j], align_bytes=64,
+            )
             nc.scalar.activation(
                 squares[:].rearrange("p t s -> p s t"),
                 diff[:].rearrange("p (s t) -> p s t", t=PACK),
@@ -109,28 +121,36 @@ def tile_attend_noveltyread_pl_kernel(tc, query, keys_words, keys_scales, bias, 
                     start=(j == 0 and t % 2 == 0), stop=(j == PACK - 1 and t % 2 == 1),
                 )
 
+        gather_values(0)
+        scale_and_weave(0, ())
+        novelty_part(0)
+        for j in range(1, PACK):
+            gather_values(j)
             if j < PACK - 1:
-                pairs = ring.tile([P, 2, P, 2], BF16, name="pairs")
-            else:
-                pairs = held.tile([P, 2, P, 2], BF16, name="last_pairs", tag="diff3", align_bytes=64)
-            for t in range(PACK):
-                nc.scalar.activation(pairs[:, t // 2, :, t % 2], va_turned[:, t, :], ACT.Copy, scale=vsc_t[:, t : t + 1])
-            if j == PACK - 1:
-                for t in range(2):
-                    nc.scalar.activation(summed[:, t, :], squares_sum[0][:, t, :], ACT.Copy, accum_out=total[:, t : t + 1])
-            nc.scalar.copy(
-                vv_bf[:, j, :].bitcast(F32).rearrange("p (e u) -> p e u", u=2),
-                pairs[:].rearrange("p u e r -> p u (e r)").bitcast(F32).rearrange("p u e -> p e u"),
-            )
+                scale_and_weave(j, ())
+        for j in range(1, PACK):
+            novelty_part(j)
+        scale_and_weave(PACK - 1, (0, 1))
 
         scales_listed = held.tile([P, I], U8, name="scales_listed", tag="va3", align_bytes=64)
         nc.vector.tensor_copy(scales_listed[:], key_scales[:].indirect(list_a[:]))
-        query_codes = held.tile([P, Q], U32, name="query_codes", tag="diff2", align_bytes=64)
+        query_codes = held.tile([P, Q], U32, name="query_codes", tag="planes0", align_bytes=64)
         query_scales = held.tile([P, Q], U8, name="query_scales", align_bytes=64)
         nc.vector.quantize_mx(query_codes[:].bitcast(FP8X4), query_scales[:], query_bf[:].rearrange("p q j -> p (q j)"))
         words_dealt = held.tile([P, PACK, P], U16, name="words_dealt", tag="pool_rows3", align_bytes=64)
         nc.vector.tensor_copy(words_dealt[:], words_listed[:].rearrange("p (s t) -> p t s", t=PACK))
-        scales_dealt = held.tile([P, PACK, P], U8, name="scales_dealt", tag="last_squares", align_bytes=64)
+        vv_codes = held.tile([P, PACK, P], U32, name="vv_codes", align_bytes=64)
+        vv_scales = held.tile([P, PACK, P], U8, name="vv_scales", align_bytes=64)
+
+        def quantise_vv(planes):
+            nc.vector.quantize_mx(
+                vv_codes[:, planes, :].rearrange("p j e -> p (j e)").bitcast(FP8X4),
+                vv_scales[:, planes, :].rearrange("p j e -> p (j e)"),
+                vv_bf[:, planes, :].rearrange("p j x -> p (j x)"),
+            )
+
+        quantise_vv(slice(0, 2))
+        scales_dealt = held.tile([P, PACK, P], U8, name="scales_dealt", tag="pool_rows1", align_bytes=64)
         nc.vector.tensor_copy(scales_dealt[:], scales_listed[:].rearrange("p (s t) -> p t s", t=PACK))
 
         sig = []
@@ -154,18 +174,11 @@ def tile_attend_noveltyread_pl_kernel(tc, query, keys_words, keys_scales, bias, 
             sig.append(gate)
 
         nc.vector.tensor_reduce(total[:, 2:4], squares_sum[1][:], mybir.AxisListType.X, ALU.add)
-        vv_codes = held.tile([P, PACK, P], U32, name="vv_codes", align_bytes=64)
-        vv_scales = held.tile([P, PACK, P], U8, name="vv_scales", align_bytes=64)
-        nc.vector.quantize_mx(
-            vv_codes[:].rearrange("p j e -> p (j e)").bitcast(FP8X4),
-            vv_scales[:].rearrange("p j e -> p (j e)"),
-            vv_bf[:].rearrange("p j x -> p (j x)"),
-        )
-
         den = held.tile([P, PACK], F32, name="den")
         nc.vector.scalar_tensor_tensor(den[:], total[:], 1.0 / E, half_t[:], ALU.mult, ALU.add)
         num = held.tile([P, PACK], F32, name="num")
         nc.vector.scalar_tensor_tensor(num[:], total[:], 1.0 / E, us_t[:], ALU.mult, ALU.mult)
+        quantise_vv(slice(2, 4))
         rec = held.tile([P, PACK], F32, name="rec")
         nc.vector.reciprocal(rec[:], den[:])
         nf = held.tile([P, PACK], F32, name="nf")

from contextlib import ExitStack

import concourse.mybir as mybir
from concourse.masks import make_identity

D, T, I, Q, E = 512, 1024, 512, 256, 512
FLOPS = 2 * D * I * Q + 2 * I * E * Q

F32 = mybir.dt.float32
BF16 = mybir.dt.bfloat16
I32 = mybir.dt.int32
U32 = mybir.dt.uint32
U16 = mybir.dt.uint16
U8 = mybir.dt.uint8
FP8X4 = mybir.dt.float8_e4m3fn_x4
FP4X4 = mybir.dt.float4_e2m1fn_x4
ALU = mybir.AluOpType
ACT = mybir.ActivationFunctionType

P = 128
PACK = 4
HALVES = 2
QH = Q // HALVES


def tile_attend_noveltyread_pl_kernel(tc, query, keys_words, keys_scales, bias, vals, half, us, vsc, offs, offs2, out_0, out_1, out_2):
    nc = tc.nc
    with ExitStack() as ctx:
        held = ctx.enter_context(tc.tile_pool(name="held", bufs=1))
        psum = ctx.enter_context(tc.psum_pool(name="psum", bufs=1))
        psum2 = ctx.enter_context(tc.psum_pool(name="psum2", bufs=2))

        list_a = held.tile([P, I // 16], U16, name="list_a")
        list_b = held.tile([P, I // 16], U16, name="list_b")
        key_scales = held.tile([P, T], U8, name="key_scales")
        key_words = held.tile([P, T], U16, name="key_words")
        pool_rows = [held.tile([P, T], F32, name=f"pool_rows{j}", tag=f"pool_rows{j}", align_bytes=64) for j in range(PACK)]
        query_raw = held.tile([P, PACK, Q], F32, name="query_raw", tag="query_raw", align_bytes=64)
        bias_t = held.tile([P, PACK], F32, name="bias_t")
        half_t = held.tile([P, PACK], F32, name="half_t")
        us_t = held.tile([P, PACK], F32, name="us_t")
        vsc_t = held.tile([P, PACK], F32, name="vsc_t")
        ident = held.tile([P, P], F32, name="ident")
        warm_in = held.tile([P, 1], F32, name="warm_in")
        warm_out = held.tile([P, 1], F32, name="warm_out")

        vals_dealt = vals.rearrange("(p j) t -> p j t", j=PACK)

        def by_slot(vec):
            return vec.rearrange("(p t) o -> p (t o)", t=PACK)

        nc.gpsimd.memset(key_scales[:].bitcast(I32), 0)
        nc.vector.memset(warm_in[:], 0.0)
        nc.sync.dma_start(list_a[:], offs)
        nc.sync.dma_start(key_words[:].bitcast(I32), keys_words[0].bitcast(I32))
        nc.scalar.activation(warm_out[:], warm_in[:], ACT.Sigmoid)
        nc.sync.dma_start(pool_rows[0][:], vals_dealt[:, 0, :])
        nc.sync.dma_start(list_b[:], offs2)
        nc.sync.dma_start(query_raw[:], query.rearrange("(p j) q -> p j q", j=PACK))
        nc.sync.dma_start(vsc_t[:], by_slot(vsc))
        for j in range(1, PACK):
            nc.sync.dma_start(pool_rows[j][:], vals_dealt[:, j, :])
        for quad in range(4):
            nc.sync.dma_start(
                key_scales[32 * quad : 32 * quad + 4, :].bitcast(I32),
                keys_scales[0, 4 * quad : 4 * quad + 4, :].bitcast(I32),
            )
        nc.sync.dma_start(bias_t[:], by_slot(bias))
        nc.sync.dma_start(half_t[:], by_slot(half))
        nc.sync.dma_start(us_t[:], by_slot(us))
        make_identity(nc, ident[:])

        words_listed = held.tile([P, I], U16, name="words_listed")
        nc.vector.tensor_copy(words_listed[:], key_words[:].indirect(list_a[:]))

        query_bf = held.tile([P, Q, PACK], BF16, name="query_bf", align_bytes=64)
        nc.scalar.copy(
            query_bf[:].rearrange("p (c i) j -> p c j i", i=4),
            query_raw[:].rearrange("p j (c i) -> p c j i", i=4),
        )

        squares_sum = [psum.tile([P, 2, P], F32, name=f"squares_sum{u}") for u in range(2)]
        vv_bf = held.tile([P, PACK, P * PACK], BF16, name="vv_bf", align_bytes=64)
        total = held.tile([P, PACK], F32, name="total")
        summed = held.tile([P, 2, P], F32, name="summed")
        listed, turned = {}, {}

        def gather_values(j):
            listed[j] = held.tile([P, I], F32, name=f"va{j}", tag=f"va{j}", align_bytes=64)
            nc.vector.tensor_copy(listed[j][:], pool_rows[j][:].indirect(list_a[:]))
            turned[j] = psum2.tile([P, PACK, P], F32, name=f"va_turned{j}", tag="va_turned")
            for t in range(PACK):
                nc.tensor.transpose(turned[j][:, t, :], listed[j][:, t::PACK], ident[:])

        def scale_and_weave(j, between):
            planes = held.tile([P, PACK, P], BF16, name=f"planes{j}", tag=("planes0", "planes1", "planes2", "pool_rows2")[j], align_bytes=64)
            for t in range(PACK):
                nc.scalar.activation(planes[:, t, :], turned[j][:, t, :], ACT.Copy, scale=vsc_t[:, t : t + 1])
            for t in between:
                nc.scalar.activation(summed[:, t, :], squares_sum[0][:, t, :], ACT.Copy, accum_out=total[:, t : t + 1])
            nc.scalar.copy(
                vv_bf[:, j, :].rearrange("p (c i t) -> p c t i", i=4, t=PACK),
                planes[:].rearrange("p t (c i) -> p c t i", i=4),
            )

        def novelty_part(j):
            diff = held.tile([P, I], F32, name=f"diff{j}", tag=("diff0", "planes0", "pool_rows1", "pool_rows2")[j], align_bytes=64)
            nc.vector.tensor_tensor(diff[:], pool_rows[j][:].indirect(list_b[:]), listed[j][:], ALU.subtract)
            squares = held.tile(
                [P, PACK, P], F32, name=f"squares{j}",
                tag=("query_raw", "planes2", "planes0", "pool_rows1")[j], align_bytes=64,
            )
            nc.scalar.activation(
                squares[:].rearrange("p t s -> p s t"),
                diff[:].rearrange("p (s t) -> p s t", t=PACK),
                ACT.Square,
            )
            for t in range(PACK):
                nc.tensor.matmul(
                    squares_sum[t // 2][:, t % 2, :], squares[:, t, :], ident[:], is_transpose=True,
                    start=(j == 0 and t % 2 == 0), stop=(j == PACK - 1 and t % 2 == 1),
                )

        gather_values(0)
        scale_and_weave(0, ())
        novelty_part(0)
        for j in range(1, PACK):
            gather_values(j)
            if j < PACK - 1:
                scale_and_weave(j, ())
        for j in range(1, PACK):
            novelty_part(j)
        scale_and_weave(PACK - 1, (0, 1))

        scales_listed = held.tile([P, I], U8, name="scales_listed", tag="va3", align_bytes=64)
        nc.vector.tensor_copy(scales_listed[:], key_scales[:].indirect(list_a[:]))
        query_codes = held.tile([P, Q], U32, name="query_codes", tag="planes0", align_bytes=64)
        query_scales = held.tile([P, Q], U8, name="query_scales", align_bytes=64)
        nc.vector.quantize_mx(query_codes[:].bitcast(FP8X4), query_scales[:], query_bf[:].rearrange("p q j -> p (q j)"))
        words_dealt = held.tile([P, PACK, P], U16, name="words_dealt", tag="pool_rows3", align_bytes=64)
        nc.vector.tensor_copy(words_dealt[:], words_listed[:].rearrange("p (s t) -> p t s", t=PACK))
        vv_codes = held.tile([P, PACK, P], U32, name="vv_codes", align_bytes=64)
        vv_scales = held.tile([P, PACK, P], U8, name="vv_scales", align_bytes=64)

        def quantise_vv(planes):
            nc.vector.quantize_mx(
                vv_codes[:, planes, :].rearrange("p j e -> p (j e)").bitcast(FP8X4),
                vv_scales[:, planes, :].rearrange("p j e -> p (j e)"),
                vv_bf[:, planes, :].rearrange("p j x -> p (j x)"),
            )

        quantise_vv(slice(0, 2))
        scales_dealt = held.tile([P, PACK, P], U8, name="scales_dealt", tag="pool_rows1", align_bytes=64)
        nc.vector.tensor_copy(scales_dealt[:], scales_listed[:].rearrange("p (s t) -> p t s", t=PACK))

        sig = []
        for h in range(HALVES):
            cols = slice(h * QH, (h + 1) * QH)
            if h == 0:
                scores = [psum.tile([P, QH], F32, name=f"scores0_{t}")[:] for t in range(PACK)]
            else:
                shared = psum2.tile([P, PACK, QH], F32, name="scores1", tag="va_turned")
                scores = [shared[:, t, :] for t in range(PACK)]
            for t in range(PACK):
                nc.tensor.matmul_mx(
                    scores[t],
                    lhsT=words_dealt[:, t, :].bitcast(FP4X4), lhsT_scale=scales_dealt[:, t, :],
                    rhs=query_codes[:, cols].bitcast(FP8X4), rhs_scale=query_scales[:, cols],
                    start=True, stop=True,
                )
            gate = held.tile([P, PACK, QH], F32, name=f"gate{h}")
            for t in range(PACK):
                nc.scalar.activation(gate[:, t, :], scores[t], ACT.Sigmoid, bias=bias_t[:, t : t + 1])
            sig.append(gate)

        nc.vector.tensor_reduce(total[:, 2:4], squares_sum[1][:], mybir.AxisListType.X, ALU.add)
        den = held.tile([P, PACK], F32, name="den")
        nc.vector.scalar_tensor_tensor(den[:], total[:], 1.0 / E, half_t[:], ALU.mult, ALU.add)
        num = held.tile([P, PACK], F32, name="num")
        nc.vector.scalar_tensor_tensor(num[:], total[:], 1.0 / E, us_t[:], ALU.mult, ALU.mult)
        quantise_vv(slice(2, 4))
        rec = held.tile([P, PACK], F32, name="rec")
        nc.vector.reciprocal(rec[:], den[:])
        nf = held.tile([P, PACK], F32, name="nf")
        nc.vector.tensor_tensor(nf[:], num[:], rec[:], ALU.mult)

        w_bf = []
        for h in range(HALVES):
            w = held.tile([P, QH, PACK], BF16, name=f"w_bf{h}", align_bytes=64)
            nc.vector.tensor_tensor(
                w[:].rearrange("p (c i) t -> p c t i", i=4),
                sig[h][:].rearrange("p t (c i) -> p c t i", i=4),
                nf[:].unsqueeze(1).unsqueeze(3).to_broadcast([P, QH // 4, PACK, 4]),
                ALU.mult,
            )
            w_bf.append(w)

        out_dealt = out_0.rearrange("(p j) q -> p j q", j=PACK)
        out_words = out_1[0].rearrange("p c r -> p (c r)").bitcast(I32)
        out_scales = held.tile([P, Q], U8, name="out_scales", align_bytes=64)
        results = []
        for h in range(HALVES):
            w_codes = held.tile([P, QH], U32, name=f"w_codes{h}", align_bytes=64)
            w_scales = held.tile([P, QH], U8, name=f"w_scales{h}", align_bytes=64)
            nc.vector.quantize_mx(w_codes[:].bitcast(FP8X4), w_scales[:], w_bf[h][:].rearrange("p q t -> p (q t)"))
            acc = psum2.tile([P, PACK, QH], F32, name=f"acc{h}", tag="va_turned")
            for j in range(PACK):
                nc.tensor.matmul_mx(
                    acc[:, j, :],
                    lhsT=vv_codes[:, j, :].bitcast(FP8X4), lhsT_scale=vv_scales[:, j, :],
                    rhs=w_codes[:].bitcast(FP8X4), rhs_scale=w_scales[:],
                    start=True, stop=True,
                )
            result = held.tile([P, PACK, QH], F32, name=f"result{h}")
            nc.scalar.copy(result[:], acc[:])
            nc.sync.dma_start(out_dealt[:, :, h * QH : (h + 1) * QH], result[:])
            results.append(result)

        for h in range(HALVES):
            cols = slice(h * QH, (h + 1) * QH)
            out_bf = held.tile([P, QH, PACK], BF16, name=f"out_bf{h}", align_bytes=64)
            nc.vector.tensor_copy(
                out_bf[:].rearrange("p (c i) j -> p c j i", i=4),
                results[h][:].rearrange("p j (c i) -> p c j i", i=4),
            )
            out_codes = held.tile([P, QH], U32, name=f"out_codes{h}", align_bytes=64)
            nc.vector.quantize_mx(out_codes[:].bitcast(FP8X4), out_scales[:, cols], out_bf[:].rearrange("p q j -> p (q j)"))
            nc.sync.dma_start(out_words[:, cols], out_codes[:].bitcast(I32))
        for quad in range(4):
            queue = nc.sync if quad % 2 == 0 else nc.scalar
            queue.dma_start(
                out_2[0, 4 * quad : 4 * quad + 4, :].bitcast(I32),
                out_scales[32 * quad : 32 * quad + 4, :].bitcast(I32),
            )
